import numpy as np, ml_dtypes
CORES = [44,45,46,47,172,173,174,175,300,301,302,303,428,429,430,431]
N = 16
F = 32
BETA, LR = 0.75, 0.5
def setup_inputs(rng):
    return {"gr": rng.standard_normal((N, 128, N * F), dtype=np.float32).astype(ml_dtypes.bfloat16), "m": rng.standard_normal((N, 128, F), dtype=np.float32).astype(ml_dtypes.bfloat16), "w": rng.standard_normal((N, 128, F), dtype=np.float32).astype(ml_dtypes.bfloat16)}
def setup_inputs_big(rng):
    d = setup_inputs(rng)
    for k in ("gr", "m", "w"): d[k] = (d[k].astype(np.float32) * 1048576.0).astype(d[k].dtype)
    return d
def setup_inputs_small(rng):
    d = setup_inputs(rng)
    for k in ("gr", "m", "w"): d[k] = (d[k].astype(np.float32) * (1 / 1048576.0)).astype(d[k].dtype)
    return d
def setup_inputs_apart(rng):
    d = setup_inputs(rng)
    f = (10.0 ** rng.permutation(np.linspace(-1.5, 1.5, N))).astype(np.float32).reshape(N, 1, 1)
    for k in ("gr", "m", "w"): d[k] = (d[k].astype(np.float32) * f).astype(d[k].dtype)
    return d
def reference(gr, m, w):
    GR, M, W = gr.astype(np.float64), m.astype(np.float64), w.astype(np.float64)
    s = GR.sum(axis=0)
    m2 = np.stack([BETA * M[r] + s[:, F * r:F * r + F] for r in range(N)])
    w2 = np.concatenate([W[r] - LR * m2[r] for r in range(N)], axis=1)
    return {"y": np.broadcast_to(w2.astype(ml_dtypes.bfloat16), (N, 128, N * F)), "mo": m2.astype(ml_dtypes.bfloat16)}

@@ -1,0 +1,155 @@
+from concourse.bass import DstId, RemoteDMATransfer
+from concourse.mybir import AluOpType
+
+F = 32
+Q = 128
+
+SCRATCH = {
+    "gsb": ("sbuf", [128, 512], "bfloat16"),
+    "z": ("sbuf", [128, 512], "bfloat16"),
+    "P": ("sbuf", [128, 512], "bfloat16"),
+    "msb": ("sbuf", [128, F], "bfloat16"),
+    "wsb": ("sbuf", [128, F], "bfloat16"),
+    "km": ("sbuf", [128, F], "bfloat16"),
+    "kh": ("psum", [128, 512], "float32"),
+    "x": ("sbuf", [128, F], "bfloat16"),
+    "b": ("sbuf", [128, F], "bfloat16"),
+    "t": ("sbuf", [128, 256], "bfloat16"),
+    "A0": ("sbuf", [128, Q], "bfloat16"),
+    "rS": ("sbuf", [128, Q], "bfloat16"),
+    "A1": ("sbuf", [128, Q], "bfloat16"),
+    "rC": ("sbuf", [128, Q], "bfloat16"),
+    "yb": ("sbuf", [128, 512], "bfloat16"),
+    "d": ("sbuf", [128, F], "bfloat16"),
+    "mob": ("sbuf", [128, F], "bfloat16"),
+}
+SEMAPHORES = ["ldg", "ldmw", "sty", "stmo", "k", "vx", "vb", "vz", "vi", "vown", "vowni", "vt", "va0", "va1", "vfull",
+              "vd", "vmo", "h1", "h2", "h3", "h4", "loc"]
+
+
+def _engines(mask):
+    return [e for e in range(mask.bit_length()) if (mask >> e) & 1]
+
+
+def _mask(engs):
+    m = 0
+    for e in engs:
+        m |= 1 << e
+    return m
+
+
+def rank_program(g, core, T, topo):
+    r = T.rank_of(core)
+    if r is None:
+        return
+    S, V = T.sem, g.vector
+    add, sub, mult = AluOpType.add, AluOpType.subtract, AluOpType.mult
+
+    byhost = {}
+    for x in T.cores:
+        byhost.setdefault(topo.host(x), []).append(x)
+    mine = byhost[topo.host(core)]
+    c = mine.index(core)
+    sw = cab = None
+    for h, lst in byhost.items():
+        if h == topo.host(core):
+            continue
+        if topo.same_plane(core, lst[c]):
+            sw = lst[c]
+        elif topo.may_write(core, lst[c]):
+            cab = lst[c]
+    sibs = [x for x in mine if x != core]
+    qb, jb = (F * r) // Q, (F * r) % Q
+
+    def dst(d):
+        rid, pid = topo.addr(d, core)
+        return DstId(rid=rid, pnc=pid)
+
+    on = _engines(topo.mask(core, sibs[0]))
+    grp = [_mask(on[4 * i:4 * i + 4]) for i in range(3)]
+    m_sw, m_cab = topo.mask(core, sw), topo.mask(core, cab)
+    n_sw, n_cab = len(_engines(m_sw)), len(_engines(m_cab))
+
+    g.sync.dma_start(T.gsb[:], T.gr[:]).then_inc(S.ldg, 16)
+    g.scalar.dma_start(T.msb[:], T.m[:]).then_inc(S.ldmw, 16)
+    g.scalar.dma_start(T.wsb[:], T.w[:]).then_inc(S.ldmw, 16)
+
+    V.memset(T.kh[:], -0.5).then_inc(S.k, 1)
+    V.memset(T.km[:], -0.375).then_inc(S.k, 1)
+    V.wait_ge(S.k, 2)
+    V.wait_ge(S.ldg, 16)
+    nz = 0
+    for lo, hi in ((0, Q * c), (Q * c + Q, 512)):
+        if hi > lo:
+            V.tensor_tensor(T.z[:, lo:hi], T.gsb[:, lo:hi], T.kh[:, lo:hi], mult).then_inc(S.vz, 1)
+            nz += 1
+    V.wait_ge(S.ldmw, 32)
+    V.tensor_tensor(T.x[:], T.msb[:], T.km[:], mult).then_inc(S.vx, 1)
+    V.wait_ge(S.vx, 1)
+    V.tensor_tensor(T.b[:], T.wsb[:], T.x[:], add).then_inc(S.vb, 1)
+    V.wait_ge(S.vb, 1)
+    if qb != c:
+        V.wait_ge(S.vz, nz)
+        V.tensor_tensor(T.z[:, F * r:F * r + F], T.z[:, F * r:F * r + F], T.b[:], add).then_inc(S.vi, 1)
+    V.tensor_tensor(T.P[:, 0:Q], T.gsb[:, Q * c:Q * c + Q], T.kh[:, Q * c:Q * c + Q], mult).then_inc(S.vown, 1)
+    V.wait_ge(S.vown, 1)
+    if qb == c:
+        V.tensor_tensor(T.P[:, jb:jb + F], T.P[:, jb:jb + F], T.b[:], add).then_inc(S.vowni, 1)
+        V.wait_ge(S.vowni, 1)
+
+    g.wait_ge(S.vz, nz)
+    if qb != c:
+        g.wait_ge(S.vi, 1)
+    tr = []
+    for i, d in enumerate(sibs):
+        cd = mine.index(d)
+        slot = 1 + [x for x in mine if x != d].index(core)
+        tr.append(RemoteDMATransfer(dst_ids=[dst(d)], dma_engine_mask=grp[i], remote_sem=S.h1,
+                                    src=T.z[:, Q * cd:Q * cd + Q], dst=T.P[:, Q * slot:Q * slot + Q]))
+    g.remote_dma_fused(tr, local_sem=S.loc)
+
+    g.wait_ge(S.h1, 12)
+    g.wait_ge(S.vown, 1)
+    if qb == c:
+        g.wait_ge(S.vowni, 1)
+    g.remote_dma_fused([RemoteDMATransfer(dst_ids=[dst(sw)], dma_engine_mask=m_sw, remote_sem=S.h2, alu_op=1,
+                                          srcs=[T.P[:, Q * i:Q * i + Q] for i in range(4)], dsts=[T.rS[:]])],
+                       local_sem=S.loc)
+    V.wait_ge(S.h1, 12)
+    V.tensor_tensor(T.t[:], T.P[:, 0:256], T.P[:, 256:512], add).then_inc(S.vt, 1)
+    V.wait_ge(S.vt, 1)
+    V.tensor_tensor(T.A0[:], T.t[:, 0:Q], T.t[:, Q:2 * Q], add).then_inc(S.va0, 1)
+
+    g.wait_ge(S.h2, n_sw)
+    g.wait_ge(S.va0, 1)
+    g.remote_dma_fused([RemoteDMATransfer(dst_ids=[dst(cab)], dma_engine_mask=m_cab, remote_sem=S.h3, alu_op=1,
+                                          srcs=[T.A0[:], T.rS[:]], dsts=[T.rC[:]])], local_sem=S.loc)
+    V.wait_ge(S.h2, n_sw)
+    V.wait_ge(S.va0, 1)
+    V.tensor_tensor(T.A1[:], T.A0[:], T.rS[:], add).then_inc(S.va1, 1)
+
+    g.wait_ge(S.h3, n_cab)
+    g.wait_ge(S.va1, 1)
+    g.remote_dma_fused([RemoteDMATransfer(dst_ids=[dst(d)], dma_engine_mask=grp[i], remote_sem=S.h4, alu_op=1,
+                                          srcs=[T.A1[:], T.rC[:]], dsts=[T.yb[:, Q * c:Q * c + Q]])
+                        for i, d in enumerate(sibs)], local_sem=S.loc)
+    V.wait_ge(S.h3, n_cab)
+    V.wait_ge(S.va1, 1)
+    V.tensor_tensor(T.yb[:, Q * c:Q * c + Q], T.A1[:], T.rC[:], add).then_inc(S.vfull, 1)
+
+    g.sync.wait_ge(S.vfull, 1)
+    g.sync.wait_ge(S.h4, 12)
+    g.sync.dma_start(T.y[:], T.yb[:]).then_inc(S.sty, 16)
+    g.sync.wait_ge(S.sty, 16)
+
+    V.wait_ge(S.vfull, 1)
+    if qb != c:
+        V.wait_ge(S.h4, 12)
+    V.tensor_tensor(T.d[:], T.wsb[:], T.yb[:, F * r:F * r + F], sub).then_inc(S.vd, 1)
+    V.wait_ge(S.vd, 1)
+    V.tensor_tensor(T.mob[:], T.d[:], T.d[:], add).then_inc(S.vmo, 1)
+    g.scalar.wait_ge(S.vmo, 1)
+    g.scalar.dma_start(T.mo[:], T.mob[:]).then_inc(S.stmo, 16)
+    g.scalar.wait_ge(S.stmo, 16)
+
+    g.wait_ge(S.loc, 12 + n_sw + n_cab + 12)

@@ -6,25 +6,31 @@ Q = 128
 
 SCRATCH = {
     "gsb": ("sbuf", [128, 512], "bfloat16"),
-    "z": ("sbuf", [128, 512], "bfloat16"),
-    "P": ("sbuf", [128, 512], "bfloat16"),
+    "L": ("sbuf", [128, 3 * Q], "bfloat16"),
+    "bq": ("sbuf", [128, Q], "bfloat16"),
     "msb": ("sbuf", [128, F], "bfloat16"),
     "wsb": ("sbuf", [128, F], "bfloat16"),
     "km": ("sbuf", [128, F], "bfloat16"),
-    "kh": ("psum", [128, 512], "float32"),
+    "khs": ("sbuf", [128, Q], "bfloat16"),
+    "kh": ("psum", [128, Q], "float32"),
+    "p1": ("psum", [128, Q], "float32"),
+    "p2": ("psum", [128, Q], "float32"),
+    "p3": ("psum", [128, Q], "float32"),
+    "p4": ("psum", [128, Q], "float32"),
     "x": ("sbuf", [128, F], "bfloat16"),
     "b": ("sbuf", [128, F], "bfloat16"),
-    "t": ("sbuf", [128, 256], "bfloat16"),
+    "o1": ("sbuf", [128, Q], "bfloat16"),
     "A0": ("sbuf", [128, Q], "bfloat16"),
     "rS": ("sbuf", [128, Q], "bfloat16"),
+    "rSs": ("sbuf", [128, Q], "bfloat16"),
     "A1": ("sbuf", [128, Q], "bfloat16"),
     "rC": ("sbuf", [128, Q], "bfloat16"),
     "yb": ("sbuf", [128, 512], "bfloat16"),
     "d": ("sbuf", [128, F], "bfloat16"),
     "mob": ("sbuf", [128, F], "bfloat16"),
 }
-SEMAPHORES = ["ldg", "ldmw", "sty", "stmo", "k", "vx", "vb", "vz", "vi", "vown", "vowni", "vt", "va0", "va1", "vfull",
-              "vd", "vmo", "h1", "h2", "h3", "h4", "loc"]
+SEMAPHORES = ["ldg", "ldmw", "sty", "stmo", "k", "vx", "vb", "vo", "s1", "s2", "s3", "s4", "va0", "vr", "va1", "vfull",
+              "vd", "vmo", "h1", "hb", "h2", "h3", "h4", "loc"]
 
 
 def _engines(mask):
@@ -59,7 +65,11 @@ def rank_program(g, core, T, topo):
         elif topo.may_write(core, lst[c]):
             cab = lst[c]
     sibs = [x for x in mine if x != core]
+    swh = byhost[topo.host(sw)]
     qb, jb = (F * r) // Q, (F * r) % Q
+    qs = (F * T.rank_of(sw)) // Q
+    own = slice(Q * c, Q * c + Q)
+    blk = slice(F * r, F * r + F)
 
     def dst(d):
         rid, pid = topo.addr(d, core)
@@ -69,73 +79,88 @@ def rank_program(g, core, T, topo):
     grp = [_mask(on[4 * i:4 * i + 4]) for i in range(3)]
     m_sw, m_cab = topo.mask(core, sw), topo.mask(core, cab)
     n_sw, n_cab = len(_engines(m_sw)), len(_engines(m_cab))
+    m_bon = grp[2]
+    n_loc = 0
 
     g.sync.dma_start(T.gsb[:], T.gr[:]).then_inc(S.ldg, 16)
     g.scalar.dma_start(T.msb[:], T.m[:]).then_inc(S.ldmw, 16)
     g.scalar.dma_start(T.wsb[:], T.w[:]).then_inc(S.ldmw, 16)
 
-    V.memset(T.kh[:], -0.5).then_inc(S.k, 1)
-    V.memset(T.km[:], -0.375).then_inc(S.k, 1)
-    V.wait_ge(S.k, 2)
-    V.wait_ge(S.ldg, 16)
-    nz = 0
-    for lo, hi in ((0, Q * c), (Q * c + Q, 512)):
-        if hi > lo:
-            V.tensor_tensor(T.z[:, lo:hi], T.gsb[:, lo:hi], T.kh[:, lo:hi], mult).then_inc(S.vz, 1)
-            nz += 1
-    V.wait_ge(S.ldmw, 32)
-    V.tensor_tensor(T.x[:], T.msb[:], T.km[:], mult).then_inc(S.vx, 1)
-    V.wait_ge(S.vx, 1)
-    V.tensor_tensor(T.b[:], T.wsb[:], T.x[:], add).then_inc(S.vb, 1)
-    V.wait_ge(S.vb, 1)
-    if qb != c:
-        V.wait_ge(S.vz, nz)
-        V.tensor_tensor(T.z[:, F * r:F * r + F], T.z[:, F * r:F * r + F], T.b[:], add).then_inc(S.vi, 1)
-    V.tensor_tensor(T.P[:, 0:Q], T.gsb[:, Q * c:Q * c + Q], T.kh[:, Q * c:Q * c + Q], mult).then_inc(S.vown, 1)
-    V.wait_ge(S.vown, 1)
-    if qb == c:
-        V.tensor_tensor(T.P[:, jb:jb + F], T.P[:, jb:jb + F], T.b[:], add).then_inc(S.vowni, 1)
-        V.wait_ge(S.vowni, 1)
-
-    g.wait_ge(S.vz, nz)
-    if qb != c:
-        g.wait_ge(S.vi, 1)
+    g.wait_ge(S.ldg, 16)
     tr = []
     for i, d in enumerate(sibs):
         cd = mine.index(d)
-        slot = 1 + [x for x in mine if x != d].index(core)
+        slot = [x for x in mine if x != d].index(core)
         tr.append(RemoteDMATransfer(dst_ids=[dst(d)], dma_engine_mask=grp[i], remote_sem=S.h1,
-                                    src=T.z[:, Q * cd:Q * cd + Q], dst=T.P[:, Q * slot:Q * slot + Q]))
+                                    src=T.gsb[:, Q * cd:Q * cd + Q], dst=T.L[:, Q * slot:Q * slot + Q]))
     g.remote_dma_fused(tr, local_sem=S.loc)
+    n_loc += 12
+
+    V.memset(T.kh[:], -0.5).then_inc(S.k, 1)
+    V.memset(T.khs[:], -0.5).then_inc(S.k, 1)
+    V.memset(T.km[:], -0.375).then_inc(S.k, 1)
+    V.wait_ge(S.k, 3)
+    V.wait_ge(S.ldmw, 32)
+    V.tensor_tensor(T.x[:], T.msb[:], T.km[:], mult).then_inc(S.vx, 1)
+    V.wait_ge(S.vx, 1)
+    bsrc = T.bq[:, jb:jb + F] if c == qb else T.b[:]
+    V.tensor_tensor(bsrc, T.wsb[:], T.x[:], add).then_inc(S.vb, 1)
+    V.wait_ge(S.ldg, 16)
+    V.tensor_tensor(T.o1[:], T.gsb[:, own], T.kh[:], mult).then_inc(S.vo, 1)
+
+    g.wait_ge(S.vb, 1)
+    tr = [RemoteDMATransfer(dst_ids=[dst(swh[qb])], dma_engine_mask=m_sw, remote_sem=S.hb,
+                            src=bsrc, dst=T.bq[:, jb:jb + F])]
+    n_loc += n_sw
+    if c != qb:
+        tr.append(RemoteDMATransfer(dst_ids=[dst(mine[qb])], dma_engine_mask=m_bon, remote_sem=S.hb,
+                                    src=bsrc, dst=T.bq[:, jb:jb + F]))
+        n_loc += 4
+    g.remote_dma_fused(tr, local_sem=S.loc)
+    n_hb = 3 * 4 if c == qb else (4 * n_sw if c == qs else 0)
 
     g.wait_ge(S.h1, 12)
-    g.wait_ge(S.vown, 1)
-    if qb == c:
-        g.wait_ge(S.vowni, 1)
     g.remote_dma_fused([RemoteDMATransfer(dst_ids=[dst(sw)], dma_engine_mask=m_sw, remote_sem=S.h2, alu_op=1,
-                                          srcs=[T.P[:, Q * i:Q * i + Q] for i in range(4)], dsts=[T.rS[:]])],
-                       local_sem=S.loc)
+                                          srcs=[T.gsb[:, own]] + [T.L[:, Q * i:Q * i + Q] for i in range(3)],
+                                          dsts=[T.rS[:]])], local_sem=S.loc)
+    n_loc += n_sw
     V.wait_ge(S.h1, 12)
-    V.tensor_tensor(T.t[:], T.P[:, 0:256], T.P[:, 256:512], add).then_inc(S.vt, 1)
-    V.wait_ge(S.vt, 1)
-    V.tensor_tensor(T.A0[:], T.t[:, 0:Q], T.t[:, Q:2 * Q], add).then_inc(S.va0, 1)
+    V.tensor_tensor(T.p1[:], T.L[:, 0:Q], T.L[:, Q:2 * Q], add).then_inc(S.s1, 1)
+    V.wait_ge(S.s1, 1)
+    V.tensor_tensor(T.p2[:], T.p1[:], T.L[:, 2 * Q:3 * Q], add).then_inc(S.s2, 1)
+    V.wait_ge(S.s2, 1)
+    V.tensor_tensor(T.p3[:], T.p2[:], T.khs[:], mult).then_inc(S.s3, 1)
+    V.wait_ge(S.s3, 1)
+    V.wait_ge(S.vo, 1)
+    if n_hb:
+        V.tensor_tensor(T.p4[:], T.p3[:], T.o1[:], add).then_inc(S.s4, 1)
+        V.wait_ge(S.s4, 1)
+        V.wait_ge(S.hb, n_hb)
+        V.wait_ge(S.vb, 1)
+        V.tensor_tensor(T.A0[:], T.p4[:], T.bq[:], add).then_inc(S.va0, 1)
+    else:
+        V.tensor_tensor(T.A0[:], T.p3[:], T.o1[:], add).then_inc(S.va0, 1)
 
-    g.wait_ge(S.h2, n_sw)
-    g.wait_ge(S.va0, 1)
-    g.remote_dma_fused([RemoteDMATransfer(dst_ids=[dst(cab)], dma_engine_mask=m_cab, remote_sem=S.h3, alu_op=1,
-                                          srcs=[T.A0[:], T.rS[:]], dsts=[T.rC[:]])], local_sem=S.loc)
     V.wait_ge(S.h2, n_sw)
+    V.tensor_tensor(T.rSs[:], T.rS[:], T.kh[:], mult).then_inc(S.vr, 1)
+    g.wait_ge(S.va0, 1)
+    g.wait_ge(S.vr, 1)
+    g.remote_dma_fused([RemoteDMATransfer(dst_ids=[dst(cab)], dma_engine_mask=m_cab, remote_sem=S.h3, alu_op=1,
+                                          srcs=[T.A0[:], T.rSs[:]], dsts=[T.rC[:]])], local_sem=S.loc)
+    n_loc += n_cab
     V.wait_ge(S.va0, 1)
-    V.tensor_tensor(T.A1[:], T.A0[:], T.rS[:], add).then_inc(S.va1, 1)
+    V.wait_ge(S.vr, 1)
+    V.tensor_tensor(T.A1[:], T.A0[:], T.rSs[:], add).then_inc(S.va1, 1)
 
     g.wait_ge(S.h3, n_cab)
     g.wait_ge(S.va1, 1)
     g.remote_dma_fused([RemoteDMATransfer(dst_ids=[dst(d)], dma_engine_mask=grp[i], remote_sem=S.h4, alu_op=1,
-                                          srcs=[T.A1[:], T.rC[:]], dsts=[T.yb[:, Q * c:Q * c + Q]])
+                                          srcs=[T.A1[:], T.rC[:]], dsts=[T.yb[:, own]])
                         for i, d in enumerate(sibs)], local_sem=S.loc)
+    n_loc += 12
     V.wait_ge(S.h3, n_cab)
     V.wait_ge(S.va1, 1)
-    V.tensor_tensor(T.yb[:, Q * c:Q * c + Q], T.A1[:], T.rC[:], add).then_inc(S.vfull, 1)
+    V.tensor_tensor(T.yb[:, own], T.A1[:], T.rC[:], add).then_inc(S.vfull, 1)
 
     g.sync.wait_ge(S.vfull, 1)
     g.sync.wait_ge(S.h4, 12)
@@ -145,11 +170,11 @@ def rank_program(g, core, T, topo):
     V.wait_ge(S.vfull, 1)
     if qb != c:
         V.wait_ge(S.h4, 12)
-    V.tensor_tensor(T.d[:], T.wsb[:], T.yb[:, F * r:F * r + F], sub).then_inc(S.vd, 1)
+    V.tensor_tensor(T.d[:], T.wsb[:], T.yb[:, blk], sub).then_inc(S.vd, 1)
     V.wait_ge(S.vd, 1)
     V.tensor_tensor(T.mob[:], T.d[:], T.d[:], add).then_inc(S.vmo, 1)
     g.scalar.wait_ge(S.vmo, 1)
     g.scalar.dma_start(T.mo[:], T.mob[:]).then_inc(S.stmo, 16)
     g.scalar.wait_ge(S.stmo, 16)
 
-    g.wait_ge(S.loc, 12 + n_sw + n_cab + 12)
+    g.wait_ge(S.loc, n_loc)

@@ -29,8 +29,8 @@ SCRATCH = {
     "d": ("sbuf", [128, F], "bfloat16"),
     "mob": ("sbuf", [128, F], "bfloat16"),
 }
-SEMAPHORES = ["ldg", "ldmw", "sty", "stmo", "k", "vx", "vb", "vo", "s1", "s2", "s3", "s4", "va0", "vr", "va1", "vfull",
-              "vd", "vmo", "h1", "hb", "h2", "h3", "h4", "loc"]
+SEMAPHORES = ["ldg", "ldmw", "sty", "stmo", "k0", "k", "vx", "vb", "vo", "s1", "s2", "s3", "s4", "va0", "vr", "va1",
+              "vfull", "vd", "vmo", "h1", "hb", "h2", "h3", "h4", "loc"]
 
 
 def _engines(mask):
@@ -56,35 +56,58 @@ def rank_program(g, core, T, topo):
         byhost.setdefault(topo.host(x), []).append(x)
     mine = byhost[topo.host(core)]
     c = mine.index(core)
-    sw = cab = None
+    swh = cabh = None
     for h, lst in byhost.items():
         if h == topo.host(core):
             continue
         if topo.same_plane(core, lst[c]):
-            sw = lst[c]
+            swh = lst
         elif topo.may_write(core, lst[c]):
-            cab = lst[c]
+            cabh = lst
     sibs = [x for x in mine if x != core]
-    swh = byhost[topo.host(sw)]
     qb, jb = (F * r) // Q, (F * r) % Q
-    qs = (F * T.rank_of(sw)) // Q
     own = slice(Q * c, Q * c + Q)
     blk = slice(F * r, F * r + F)
+
+    def first(q):
+        return swh if q % 2 == 0 else cabh
+
+    def second(q):
+        return cabh if q % 2 == 0 else swh
 
     def dst(d):
         rid, pid = topo.addr(d, core)
         return DstId(rid=rid, pnc=pid)
 
+    pa, pb = first(c)[c], second(c)[c]
     on = _engines(topo.mask(core, sibs[0]))
     grp = [_mask(on[4 * i:4 * i + 4]) for i in range(3)]
-    m_sw, m_cab = topo.mask(core, sw), topo.mask(core, cab)
-    n_sw, n_cab = len(_engines(m_sw)), len(_engines(m_cab))
-    m_bon = grp[2]
+    m_off = topo.mask(core, pa) & topo.mask(core, pb)
+    n_off = len(_engines(m_off))
     n_loc = 0
+    bsrc = T.bq[:, jb:jb + F] if c == qb else T.b[:]
+    if c == qb:
+        n_hb = 3 * 4
+    elif c == (F * T.rank_of(pa)) // Q:
+        n_hb = 4 * n_off
+    else:
+        n_hb = 0
 
     g.sync.dma_start(T.gsb[:], T.gr[:]).then_inc(S.ldg, 16)
     g.scalar.dma_start(T.msb[:], T.m[:]).then_inc(S.ldmw, 16)
     g.scalar.dma_start(T.wsb[:], T.w[:]).then_inc(S.ldmw, 16)
+
+    V.memset(T.km[:], -0.375).then_inc(S.k0, 1)
+    V.wait_ge(S.k0, 1)
+    V.wait_ge(S.ldmw, 32)
+    V.tensor_tensor(T.x[:], T.msb[:], T.km[:], mult).then_inc(S.vx, 1)
+    V.wait_ge(S.vx, 1)
+    V.tensor_tensor(bsrc, T.wsb[:], T.x[:], add).then_inc(S.vb, 1)
+    V.memset(T.kh[:], -0.5).then_inc(S.k, 1)
+    V.memset(T.khs[:], -0.5).then_inc(S.k, 1)
+    V.wait_ge(S.k, 2)
+    V.wait_ge(S.ldg, 16)
+    V.tensor_tensor(T.o1[:], T.gsb[:, own], T.kh[:], mult).then_inc(S.vo, 1)
 
     g.wait_ge(S.ldg, 16)
     tr = []
@@ -96,34 +119,21 @@ def rank_program(g, core, T, topo):
     g.remote_dma_fused(tr, local_sem=S.loc)
     n_loc += 12
 
-    V.memset(T.kh[:], -0.5).then_inc(S.k, 1)
-    V.memset(T.khs[:], -0.5).then_inc(S.k, 1)
-    V.memset(T.km[:], -0.375).then_inc(S.k, 1)
-    V.wait_ge(S.k, 3)
-    V.wait_ge(S.ldmw, 32)
-    V.tensor_tensor(T.x[:], T.msb[:], T.km[:], mult).then_inc(S.vx, 1)
-    V.wait_ge(S.vx, 1)
-    bsrc = T.bq[:, jb:jb + F] if c == qb else T.b[:]
-    V.tensor_tensor(bsrc, T.wsb[:], T.x[:], add).then_inc(S.vb, 1)
-    V.wait_ge(S.ldg, 16)
-    V.tensor_tensor(T.o1[:], T.gsb[:, own], T.kh[:], mult).then_inc(S.vo, 1)
-
     g.wait_ge(S.vb, 1)
-    tr = [RemoteDMATransfer(dst_ids=[dst(swh[qb])], dma_engine_mask=m_sw, remote_sem=S.hb,
+    tr = [RemoteDMATransfer(dst_ids=[dst(first(qb)[qb])], dma_engine_mask=m_off, remote_sem=S.hb,
                             src=bsrc, dst=T.bq[:, jb:jb + F])]
-    n_loc += n_sw
+    n_loc += n_off
     if c != qb:
-        tr.append(RemoteDMATransfer(dst_ids=[dst(mine[qb])], dma_engine_mask=m_bon, remote_sem=S.hb,
+        tr.append(RemoteDMATransfer(dst_ids=[dst(mine[qb])], dma_engine_mask=grp[2], remote_sem=S.hb,
                                     src=bsrc, dst=T.bq[:, jb:jb + F]))
         n_loc += 4
     g.remote_dma_fused(tr, local_sem=S.loc)
-    n_hb = 3 * 4 if c == qb else (4 * n_sw if c == qs else 0)
 
     g.wait_ge(S.h1, 12)
-    g.remote_dma_fused([RemoteDMATransfer(dst_ids=[dst(sw)], dma_engine_mask=m_sw, remote_sem=S.h2, alu_op=1,
+    g.remote_dma_fused([RemoteDMATransfer(dst_ids=[dst(pa)], dma_engine_mask=m_off, remote_sem=S.h2, alu_op=1,
                                           srcs=[T.gsb[:, own]] + [T.L[:, Q * i:Q * i + Q] for i in range(3)],
                                           dsts=[T.rS[:]])], local_sem=S.loc)
-    n_loc += n_sw
+    n_loc += n_off
     V.wait_ge(S.h1, 12)
     V.tensor_tensor(T.p1[:], T.L[:, 0:Q], T.L[:, Q:2 * Q], add).then_inc(S.s1, 1)
     V.wait_ge(S.s1, 1)
@@ -141,24 +151,24 @@ def rank_program(g, core, T, topo):
     else:
         V.tensor_tensor(T.A0[:], T.p3[:], T.o1[:], add).then_inc(S.va0, 1)
 
-    V.wait_ge(S.h2, n_sw)
+    V.wait_ge(S.h2, n_off)
     V.tensor_tensor(T.rSs[:], T.rS[:], T.kh[:], mult).then_inc(S.vr, 1)
     g.wait_ge(S.va0, 1)
     g.wait_ge(S.vr, 1)
-    g.remote_dma_fused([RemoteDMATransfer(dst_ids=[dst(cab)], dma_engine_mask=m_cab, remote_sem=S.h3, alu_op=1,
+    g.remote_dma_fused([RemoteDMATransfer(dst_ids=[dst(pb)], dma_engine_mask=m_off, remote_sem=S.h3, alu_op=1,
                                           srcs=[T.A0[:], T.rSs[:]], dsts=[T.rC[:]])], local_sem=S.loc)
-    n_loc += n_cab
+    n_loc += n_off
     V.wait_ge(S.va0, 1)
     V.wait_ge(S.vr, 1)
     V.tensor_tensor(T.A1[:], T.A0[:], T.rSs[:], add).then_inc(S.va1, 1)
 
-    g.wait_ge(S.h3, n_cab)
+    g.wait_ge(S.h3, n_off)
     g.wait_ge(S.va1, 1)
     g.remote_dma_fused([RemoteDMATransfer(dst_ids=[dst(d)], dma_engine_mask=grp[i], remote_sem=S.h4, alu_op=1,
                                           srcs=[T.A1[:], T.rC[:]], dsts=[T.yb[:, own]])
                         for i, d in enumerate(sibs)], local_sem=S.loc)
     n_loc += 12
-    V.wait_ge(S.h3, n_cab)
+    V.wait_ge(S.h3, n_off)
     V.wait_ge(S.va1, 1)
     V.tensor_tensor(T.yb[:, own], T.A1[:], T.rC[:], add).then_inc(S.vfull, 1)
 

@@ -80,22 +80,30 @@ def rank_program(g, core, T, topo):
         return DstId(rid=rid, pnc=pid)
 
     pa, pb = first(c)[c], second(c)[c]
-    on = _engines(topo.mask(core, sibs[0]))
-    grp = [_mask(on[4 * i:4 * i + 4]) for i in range(3)]
+    m_on = topo.mask(core, sibs[0])
+    on = _engines(m_on)
+    n_on = len(on)
+    ng = n_on // 4
+    grp = [_mask(on[ng * i:ng * i + ng]) for i in range(4)]
     m_off = topo.mask(core, pa) & topo.mask(core, pb)
     n_off = len(_engines(m_off))
+    if c == qb:
+        idle = [x for x in grp if x & m_off == x][0]
+    else:
+        idle = [x for x in grp if x & m_off == 0][-1]
+    h1g = [x for x in grp if x != idle]
     n_loc = 0
     bsrc = T.bq[:, jb:jb + F] if c == qb else T.b[:]
     if c == qb:
-        n_hb = 3 * 4
+        n_hb = 3 * ng
     elif c == (F * T.rank_of(pa)) // Q:
         n_hb = 4 * n_off
     else:
         n_hb = 0
 
     g.sync.dma_start(T.gsb[:], T.gr[:]).then_inc(S.ldg, 16)
-    g.scalar.dma_start(T.msb[:], T.m[:]).then_inc(S.ldmw, 16)
-    g.scalar.dma_start(T.wsb[:], T.w[:]).then_inc(S.ldmw, 16)
+    g.sync.dma_start(T.msb[:], T.m[:]).then_inc(S.ldmw, 16)
+    g.sync.dma_start(T.wsb[:], T.w[:]).then_inc(S.ldmw, 16)
 
     V.memset(T.km[:], -0.375).then_inc(S.k0, 1)
     V.wait_ge(S.k0, 1)
@@ -114,27 +122,27 @@ def rank_program(g, core, T, topo):
     for i, d in enumerate(sibs):
         cd = mine.index(d)
         slot = [x for x in mine if x != d].index(core)
-        tr.append(RemoteDMATransfer(dst_ids=[dst(d)], dma_engine_mask=grp[i], remote_sem=S.h1,
+        tr.append(RemoteDMATransfer(dst_ids=[dst(d)], dma_engine_mask=h1g[i], remote_sem=S.h1,
                                     src=T.gsb[:, Q * cd:Q * cd + Q], dst=T.L[:, Q * slot:Q * slot + Q]))
     g.remote_dma_fused(tr, local_sem=S.loc)
-    n_loc += 12
+    n_loc += 3 * ng
 
     g.wait_ge(S.vb, 1)
     tr = [RemoteDMATransfer(dst_ids=[dst(first(qb)[qb])], dma_engine_mask=m_off, remote_sem=S.hb,
                             src=bsrc, dst=T.bq[:, jb:jb + F])]
     n_loc += n_off
     if c != qb:
-        tr.append(RemoteDMATransfer(dst_ids=[dst(mine[qb])], dma_engine_mask=grp[2], remote_sem=S.hb,
+        tr.append(RemoteDMATransfer(dst_ids=[dst(mine[qb])], dma_engine_mask=idle, remote_sem=S.hb,
                                     src=bsrc, dst=T.bq[:, jb:jb + F]))
-        n_loc += 4
+        n_loc += ng
     g.remote_dma_fused(tr, local_sem=S.loc)
 
-    g.wait_ge(S.h1, 12)
+    g.wait_ge(S.h1, 3 * ng)
     g.remote_dma_fused([RemoteDMATransfer(dst_ids=[dst(pa)], dma_engine_mask=m_off, remote_sem=S.h2, alu_op=1,
                                           srcs=[T.gsb[:, own]] + [T.L[:, Q * i:Q * i + Q] for i in range(3)],
                                           dsts=[T.rS[:]])], local_sem=S.loc)
     n_loc += n_off
-    V.wait_ge(S.h1, 12)
+    V.wait_ge(S.h1, 3 * ng)
     V.tensor_tensor(T.p1[:], T.L[:, 0:Q], T.L[:, Q:2 * Q], add).then_inc(S.s1, 1)
     V.wait_ge(S.s1, 1)
     V.tensor_tensor(T.p2[:], T.p1[:], T.L[:, 2 * Q:3 * Q], add).then_inc(S.s2, 1)
@@ -164,22 +172,22 @@ def rank_program(g, core, T, topo):
 
     g.wait_ge(S.h3, n_off)
     g.wait_ge(S.va1, 1)
-    g.remote_dma_fused([RemoteDMATransfer(dst_ids=[dst(d)], dma_engine_mask=grp[i], remote_sem=S.h4, alu_op=1,
-                                          srcs=[T.A1[:], T.rC[:]], dsts=[T.yb[:, own]])
-                        for i, d in enumerate(sibs)], local_sem=S.loc)
-    n_loc += 12
+    g.remote_dma_fused([RemoteDMATransfer(dst_ids=[dst(d) for d in sibs], dma_engine_mask=m_on, remote_sem=S.h4,
+                                          alu_op=1, srcs=[T.A1[:], T.rC[:]], dsts=[T.yb[:, own] for d in sibs])],
+                       local_sem=S.loc)
+    n_loc += n_on
     V.wait_ge(S.h3, n_off)
     V.wait_ge(S.va1, 1)
     V.tensor_tensor(T.yb[:, own], T.A1[:], T.rC[:], add).then_inc(S.vfull, 1)
 
     g.sync.wait_ge(S.vfull, 1)
-    g.sync.wait_ge(S.h4, 12)
+    g.sync.wait_ge(S.h4, 3 * n_on)
     g.sync.dma_start(T.y[:], T.yb[:]).then_inc(S.sty, 16)
     g.sync.wait_ge(S.sty, 16)
 
     V.wait_ge(S.vfull, 1)
     if qb != c:
-        V.wait_ge(S.h4, 12)
+        V.wait_ge(S.h4, 3 * n_on)
     V.tensor_tensor(T.d[:], T.wsb[:], T.yb[:, blk], sub).then_inc(S.vd, 1)
     V.wait_ge(S.vd, 1)
     V.tensor_tensor(T.mob[:], T.d[:], T.d[:], add).then_inc(S.vmo, 1)

from concourse.bass import DstId, RemoteDMATransfer
from concourse.mybir import AluOpType

F = 32
Q = 128

SCRATCH = {
    "gsb": ("sbuf", [128, 512], "bfloat16"),
    "L": ("sbuf", [128, 3 * Q], "bfloat16"),
    "bq": ("sbuf", [128, Q], "bfloat16"),
    "msb": ("sbuf", [128, F], "bfloat16"),
    "wsb": ("sbuf", [128, F], "bfloat16"),
    "km": ("sbuf", [128, F], "bfloat16"),
    "khs": ("sbuf", [128, Q], "bfloat16"),
    "kh": ("psum", [128, Q], "float32"),
    "p1": ("psum", [128, Q], "float32"),
    "p2": ("psum", [128, Q], "float32"),
    "p3": ("psum", [128, Q], "float32"),
    "p4": ("psum", [128, Q], "float32"),
    "x": ("sbuf", [128, F], "bfloat16"),
    "b": ("sbuf", [128, F], "bfloat16"),
    "o1": ("sbuf", [128, Q], "bfloat16"),
    "A0": ("sbuf", [128, Q], "bfloat16"),
    "rS": ("sbuf", [128, Q], "bfloat16"),
    "rSs": ("sbuf", [128, Q], "bfloat16"),
    "A1": ("sbuf", [128, Q], "bfloat16"),
    "rC": ("sbuf", [128, Q], "bfloat16"),
    "yb": ("sbuf", [128, 512], "bfloat16"),
    "d": ("sbuf", [128, F], "bfloat16"),
    "mob": ("sbuf", [128, F], "bfloat16"),
}
SEMAPHORES = ["ldg", "ldmw", "sty", "stmo", "k0", "k", "vx", "vb", "vo", "s1", "s2", "s3", "s4", "va0", "vr", "va1",
              "vfull", "vd", "vmo", "h1", "hb", "h2", "h3", "h4", "loc"]


def _engines(mask):
    return [e for e in range(mask.bit_length()) if (mask >> e) & 1]


def _mask(engs):
    m = 0
    for e in engs:
        m |= 1 << e
    return m


def rank_program(g, core, T, topo):
    r = T.rank_of(core)
    if r is None:
        return
    S, V = T.sem, g.vector
    add, sub, mult = AluOpType.add, AluOpType.subtract, AluOpType.mult

    byhost = {}
    for x in T.cores:
        byhost.setdefault(topo.host(x), []).append(x)
    mine = byhost[topo.host(core)]
    c = mine.index(core)
    swh = cabh = None
    for h, lst in byhost.items():
        if h == topo.host(core):
            continue
        if topo.same_plane(core, lst[c]):
            swh = lst
        elif topo.may_write(core, lst[c]):
            cabh = lst
    sibs = [x for x in mine if x != core]
    qb, jb = (F * r) // Q, (F * r) % Q
    own = slice(Q * c, Q * c + Q)
    blk = slice(F * r, F * r + F)

    def first(q):
        return swh if q % 2 == 0 else cabh

    def second(q):
        return cabh if q % 2 == 0 else swh

    def dst(d):
        rid, pid = topo.addr(d, core)
        return DstId(rid=rid, pnc=pid)

    pa, pb = first(c)[c], second(c)[c]
    m_on = topo.mask(core, sibs[0])
    on = _engines(m_on)
    n_on = len(on)
    ng = n_on // 4
    grp = [_mask(on[ng * i:ng * i + ng]) for i in range(4)]
    m_off = topo.mask(core, pa) & topo.mask(core, pb)
    n_off = len(_engines(m_off))
    if c == qb:
        idle = [x for x in grp if x & m_off == x][0]
    else:
        idle = [x for x in grp if x & m_off == 0][-1]
    h1g = [x for x in grp if x != idle]
    n_loc = 0
    bsrc = T.bq[:, jb:jb + F] if c == qb else T.b[:]
    if c == qb:
        n_hb = 3 * ng
    elif c == (F * T.rank_of(pa)) // Q:
        n_hb = 4 * n_off
    else:
        n_hb = 0

    g.sync.dma_start(T.gsb[:], T.gr[:]).then_inc(S.ldg, 16)
    g.sync.dma_start(T.msb[:], T.m[:]).then_inc(S.ldmw, 16)
    g.sync.dma_start(T.wsb[:], T.w[:]).then_inc(S.ldmw, 16)

    V.memset(T.km[:], -0.375).then_inc(S.k0, 1)
    V.wait_ge(S.k0, 1)
    V.wait_ge(S.ldmw, 32)
    V.tensor_tensor(T.x[:], T.msb[:], T.km[:], mult).then_inc(S.vx, 1)
    V.wait_ge(S.vx, 1)
    V.tensor_tensor(bsrc, T.wsb[:], T.x[:], add).then_inc(S.vb, 1)
    V.memset(T.kh[:], -0.5).then_inc(S.k, 1)
    V.memset(T.khs[:], -0.5).then_inc(S.k, 1)
    V.wait_ge(S.k, 2)
    V.wait_ge(S.ldg, 16)
    V.tensor_tensor(T.o1[:], T.gsb[:, own], T.kh[:], mult).then_inc(S.vo, 1)

    g.wait_ge(S.ldg, 16)
    tr = []
    for i, d in enumerate(sibs):
        cd = mine.index(d)
        slot = [x for x in mine if x != d].index(core)
        tr.append(RemoteDMATransfer(dst_ids=[dst(d)], dma_engine_mask=h1g[i], remote_sem=S.h1,
                                    src=T.gsb[:, Q * cd:Q * cd + Q], dst=T.L[:, Q * slot:Q * slot + Q]))
    g.remote_dma_fused(tr, local_sem=S.loc)
    n_loc += 3 * ng

    g.wait_ge(S.vb, 1)
    tr = [RemoteDMATransfer(dst_ids=[dst(first(qb)[qb])], dma_engine_mask=m_off, remote_sem=S.hb,
                            src=bsrc, dst=T.bq[:, jb:jb + F])]
    n_loc += n_off
    if c != qb:
        tr.append(RemoteDMATransfer(dst_ids=[dst(mine[qb])], dma_engine_mask=idle, remote_sem=S.hb,
                                    src=bsrc, dst=T.bq[:, jb:jb + F]))
        n_loc += ng
    g.remote_dma_fused(tr, local_sem=S.loc)

    g.wait_ge(S.h1, 3 * ng)
    g.remote_dma_fused([RemoteDMATransfer(dst_ids=[dst(pa)], dma_engine_mask=m_off, remote_sem=S.h2, alu_op=1,
                                          srcs=[T.gsb[:, own]] + [T.L[:, Q * i:Q * i + Q] for i in range(3)],
                                          dsts=[T.rS[:]])], local_sem=S.loc)
    n_loc += n_off
    V.wait_ge(S.h1, 3 * ng)
    V.tensor_tensor(T.p1[:], T.L[:, 0:Q], T.L[:, Q:2 * Q], add).then_inc(S.s1, 1)
    V.wait_ge(S.s1, 1)
    V.tensor_tensor(T.p2[:], T.p1[:], T.L[:, 2 * Q:3 * Q], add).then_inc(S.s2, 1)
    V.wait_ge(S.s2, 1)
    V.tensor_tensor(T.p3[:], T.p2[:], T.khs[:], mult).then_inc(S.s3, 1)
    V.wait_ge(S.s3, 1)
    V.wait_ge(S.vo, 1)
    if n_hb:
        V.tensor_tensor(T.p4[:], T.p3[:], T.o1[:], add).then_inc(S.s4, 1)
        V.wait_ge(S.s4, 1)
        V.wait_ge(S.hb, n_hb)
        V.wait_ge(S.vb, 1)
        V.tensor_tensor(T.A0[:], T.p4[:], T.bq[:], add).then_inc(S.va0, 1)
    else:
        V.tensor_tensor(T.A0[:], T.p3[:], T.o1[:], add).then_inc(S.va0, 1)

    V.wait_ge(S.h2, n_off)
    V.tensor_tensor(T.rSs[:], T.rS[:], T.kh[:], mult).then_inc(S.vr, 1)
    g.wait_ge(S.va0, 1)
    g.wait_ge(S.vr, 1)
    g.remote_dma_fused([RemoteDMATransfer(dst_ids=[dst(pb)], dma_engine_mask=m_off, remote_sem=S.h3, alu_op=1,
                                          srcs=[T.A0[:], T.rSs[:]], dsts=[T.rC[:]])], local_sem=S.loc)
    n_loc += n_off
    V.wait_ge(S.va0, 1)
    V.wait_ge(S.vr, 1)
    V.tensor_tensor(T.A1[:], T.A0[:], T.rSs[:], add).then_inc(S.va1, 1)

    g.wait_ge(S.h3, n_off)
    g.wait_ge(S.va1, 1)
    g.remote_dma_fused([RemoteDMATransfer(dst_ids=[dst(d) for d in sibs], dma_engine_mask=m_on, remote_sem=S.h4,
                                          alu_op=1, srcs=[T.A1[:], T.rC[:]], dsts=[T.yb[:, own] for d in sibs])],
                       local_sem=S.loc)
    n_loc += n_on
    V.wait_ge(S.h3, n_off)
    V.wait_ge(S.va1, 1)
    V.tensor_tensor(T.yb[:, own], T.A1[:], T.rC[:], add).then_inc(S.vfull, 1)

    g.sync.wait_ge(S.vfull, 1)
    g.sync.wait_ge(S.h4, 3 * n_on)
    g.sync.dma_start(T.y[:], T.yb[:]).then_inc(S.sty, 16)
    g.sync.wait_ge(S.sty, 16)

    V.wait_ge(S.vfull, 1)
    if qb != c:
        V.wait_ge(S.h4, 3 * n_on)
    V.tensor_tensor(T.d[:], T.wsb[:], T.yb[:, blk], sub).then_inc(S.vd, 1)
    V.wait_ge(S.vd, 1)
    V.tensor_tensor(T.mob[:], T.d[:], T.d[:], add).then_inc(S.vmo, 1)
    g.scalar.wait_ge(S.vmo, 1)
    g.scalar.dma_start(T.mo[:], T.mob[:]).then_inc(S.stmo, 16)
    g.scalar.wait_ge(S.stmo, 16)

    g.wait_ge(S.loc, n_loc)
